import numpy as np
import ml_dtypes


def mxq(x, axis, fmt="e4m3"):
    dtype, down = {"e4m3": (ml_dtypes.float8_e4m3fn, 7), "e5m2": (ml_dtypes.float8_e5m2, 14)}[fmt]
    v = np.moveaxis(np.asarray(x, np.float32).astype(ml_dtypes.bfloat16).astype(np.float64), axis, -1)
    blocks = v.reshape(v.shape[:-1] + (-1, 32))
    amax = np.abs(blocks).max(-1, keepdims=True)
    byte = np.maximum(np.where(amax > 0, np.frexp(amax)[1] - 1 + 127, 0) - down, 1)
    scale = np.exp2(byte - 127.0)
    codes = (blocks / scale).astype(np.float32).astype(dtype).astype(np.float64)
    return np.moveaxis((codes * scale).reshape(v.shape), -1, axis)


WIDE = False


def mx_kscale(k):
    if not WIDE:
        return np.ones(k)
    levels = np.array([10, -10, 5, -5, 0])
    if k % 512:
        return np.exp2(np.random.permutation(np.resize(levels, k // 32))).repeat(32)
    a = np.empty((k // 512, 16))
    for p in range(k // 512):
        a[p, :8] = np.random.permutation(np.resize(levels, 8))
        for g in range(8):
            far = levels[np.abs(levels - a[p, g]) >= 10]
            a[p, g + 8] = far[np.random.randint(len(far))]
    return np.exp2(a.ravel()).repeat(32)


BF16 = ml_dtypes.bfloat16


def bf(x):
    return np.asarray(x, np.float32).astype(BF16)


def f64(x):
    return np.asarray(x).astype(np.float64)


M, K, R, D = 2048, 1024, 1024, 512


def draw0():
    s = mx_kscale(K)
    t = mx_kscale(M)
    x = np.random.standard_normal((M, K)) * s
    c = 2.0 * np.random.standard_normal((K, R)) / np.sqrt(K) / s[:, None]
    b = 0.5 * np.random.standard_normal(R)
    mass = np.random.uniform(0.5, 1.5, M) * t
    v = np.random.standard_normal((M, D)) / np.sqrt(M) / t[:, None]
    return {"x": bf(x), "c": bf(c), "b": bf(b), "mass": bf(mass), "v": bf(v)}


def core(x, c, b, mass, v):
    score = (mxq(f64(x), 1, "e4m3") @ mxq(f64(c), 0, "e4m3")) + f64(b)
    member = 1.0 / (1.0 + np.exp(-score))
    a = member * f64(mass)[:, None]
    centre = mxq(a, 0, "e4m3").T @ mxq(f64(v), 0, "e4m3")
    return member, centre


def e4m3fn_bytes(y):
    return np.clip(np.asarray(y, np.float64), -448.0, 448.0).astype(np.float32).astype(ml_dtypes.float8_e4m3fn).view(np.uint8)


def e4m3fn_values(b):
    return np.asarray(b, np.uint8).view(ml_dtypes.float8_e4m3fn).astype(np.float64)


def setup_inputs():
    d = draw0()
    x0 = np.asarray(d['x']).astype(np.float64)
    s = (np.max(np.abs(x0), axis=(0,), keepdims=True) / 448.0).astype(np.float32)
    out = {}
    for k, v in d.items():
        if k == 'x':
            out['x_bytes'] = e4m3fn_bytes(x0 / s.astype(np.float64))
            out['x_scale'] = s
        else:
            out[k] = v
    return out


def reference(x_bytes, x_scale, c, b, mass, v):
    return core(e4m3fn_values(x_bytes) * x_scale.astype(np.float64), c, b, mass, v)

@@ -1,0 +1,385 @@
+from contextlib import ExitStack
+
+import concourse.mybir as mybir
+from concourse.masks import make_identity
+
+M, K, R, D = 2048, 1024, 1024, 512
+FLOPS = 2 * M * K * R + 2 * M * R * D
+
+F32 = mybir.dt.float32
+BF16 = mybir.dt.bfloat16
+U32 = mybir.dt.uint32
+U8 = mybir.dt.uint8
+FP8 = mybir.dt.float8_e4m3fn
+FP8X4 = mybir.dt.float8_e4m3fn_x4
+MULT = mybir.AluOpType.mult
+ADD = mybir.AluOpType.add
+SIGMOID = mybir.ActivationFunctionType.Sigmoid
+COPY = mybir.ActivationFunctionType.Copy
+
+P = 128
+GROUP = 512
+GROUPS = M // GROUP
+PASSES = K // 512
+HALF = 512
+CHUNK = 256
+V_BLOCKS = (12, 13, 14, 15)
+C_ENGINES = ("g", "s", "g", "s")
+WEIGH_COLS = 64
+V_ENGINES = ("s", "s", "s", "s")
+FINISH = ("s", "s", "s", "s", "s", "s", "s", "v")
+
+
+def tile_soft_cluster_centres_s7_kernel(tc, x_bytes, x_scale, c, b, mass, v, member_out, centre_out):
+    nc = tc.nc
+    with ExitStack() as ctx:
+        keep = ctx.enter_context(tc.tile_pool(name="keep", bufs=1))
+        wide = ctx.enter_context(tc.tile_pool(name="wide", bufs=4))
+        xgp = ctx.enter_context(tc.tile_pool(name="xgp", bufs=2))
+        cvp = ctx.enter_context(tc.tile_pool(name="cvp", bufs=6))
+        agp = ctx.enter_context(tc.tile_pool(name="agp", bufs=3))
+        zp = ctx.enter_context(tc.tile_pool(name="zp", bufs=4))
+        outp = ctx.enter_context(tc.tile_pool(name="outp", bufs=8))
+        work = ctx.enter_context(tc.psum_pool(name="work", bufs=4))
+        sums = ctx.enter_context(tc.psum_pool(name="sums", bufs=1))
+
+        x_raw = [keep.tile([P, 4, K], U8, name=f"x_raw{g}", align_bytes=64) for g in range(GROUPS)]
+        c_raw = [[keep.tile([P, 4, HALF], BF16, name=f"c_raw{q}{h}", align_bytes=64) for h in range(2)] for q in range(PASSES)]
+        v_raw = [keep.tile([P, 4, D], BF16, name=f"v_raw{g}", align_bytes=64) for g in range(GROUPS)]
+        x_codes = keep.tile([P, 4 * GROUPS, PASSES, P], U32, name="x_codes", align_bytes=64)
+        x_planes = keep.tile([P, 4 * GROUPS, PASSES, P], U8, name="x_planes", align_bytes=64)
+        c_codes = keep.tile([P, PASSES, R], U32, name="c_codes", align_bytes=64)
+        c_planes = keep.tile([P, PASSES, R], U8, name="c_planes", align_bytes=64)
+        v_codes = keep.tile([P, GROUPS, D], U32, name="v_codes", align_bytes=64)
+        v_planes = keep.tile([P, GROUPS, D], U8, name="v_planes", align_bytes=64)
+        a_codes = keep.tile([P, GROUPS, R], U32, name="a_codes", align_bytes=64)
+        a_planes = keep.tile([P, GROUPS, R], U8, name="a_planes", align_bytes=64)
+        x_scales = keep.tile([P, PASSES, 4], F32, name="x_scales")
+        masses = keep.tile([P, GROUPS, 4], BF16, name="masses")
+        b_rows = keep.tile([P, R], BF16, name="b_rows")
+        b_all = keep.tile([P, R], F32, name="b_all")
+        ones = keep.tile([P, P], BF16, name="ones")
+        ident = keep.tile([P, P], F32, name="ident")
+        spark = keep.tile([P, 1], F32, name="spark")
+
+        def load_x(g, t0, t1):
+            rows = x_bytes[g * GROUP : (g + 1) * GROUP, :].rearrange("(p t) k -> p t k", t=4)
+            nc.sync.dma_start(out=x_raw[g][:, t0:t1, :], in_=rows[:, t0:t1, :])
+
+        def load_c(q, h):
+            rows = c[q * 512 : (q + 1) * 512, h * HALF : (h + 1) * HALF].rearrange("(p t) n -> p t n", t=4)
+            nc.sync.dma_start(out=c_raw[q][h][:], in_=rows)
+
+        def load_v(g):
+            nc.sync.dma_start(out=v_raw[g][:], in_=v[g * GROUP : (g + 1) * GROUP, :].rearrange("(p t) n -> p t n", t=4))
+
+        def interleave(eng, raw):
+            grouped = cvp.tile([P, 512, 4], BF16, name="cv_grouped", align_bytes=64)
+            src = raw[:].rearrange("p t n -> p n t")
+            if eng == "v":
+                nc.vector.tensor_copy(out=grouped[:], in_=src)
+            elif eng == "s":
+                nc.scalar.copy(out=grouped[:], in_=src)
+            else:
+                nc.gpsimd.tensor_scalar(out=grouped[:], in0=src, scalar1=1.0, scalar2=0.0, op0=MULT, op1=ADD)
+            return grouped
+
+        def quantise(codes, planes, grouped):
+            nc.vector.quantize_mx(out=codes.bitcast(FP8X4), scales=planes, in_=grouped)
+
+        def quantise_c(q, h, grouped):
+            c_done.add(2 * h + q)
+            cols = slice(h * HALF, (h + 1) * HALF)
+            quantise(c_codes[:, q, cols], c_planes[:, q, cols], grouped[:].rearrange("p n t -> p (n t)"))
+
+        def quantise_v(g, grouped):
+            quantise(v_codes[:, g, :], v_planes[:, g, :], grouped[:].rearrange("p n t -> p (n t)"))
+
+        x_wide = {}
+        x_turned = {}
+        x_grouped = {}
+        x_done = set()
+        c_done = set()
+
+        def widen(j):
+            g, t = j // 4, j % 4
+            w = wide.tile([P, K], BF16, name="x_wide")
+            nc.scalar.activation(out=w[:], in_=x_raw[g][:, t, :].bitcast(FP8), func=COPY)
+            x_wide[j] = w
+
+        def turn(j):
+            words = x_wide[j][:].bitcast(F32)
+            bank = work.tile([P, 2, PASSES, P], F32, name="bank")
+            for u in range(2):
+                for q in range(PASSES):
+                    nc.tensor.transpose(bank[:, u, q, :], words[:, q * 256 + u : (q + 1) * 256 : 2], ident[:])
+            x_turned[j] = bank
+
+        b_banks = {}
+
+        def spread_b(h):
+            b_banks[h] = work.tile([P, HALF], F32, name="bank")
+            nc.tensor.matmul(out=b_banks[h][:], lhsT=ones[:], rhs=b_rows[:, h * HALF : (h + 1) * HALF], start=True, stop=True)
+
+        def scale_x(j):
+            if j % 2 == 0:
+                x_grouped[j // 2] = xgp.tile([P, 2, PASSES, P, 4], BF16, name="x_grouped", align_bytes=64)
+            dst = x_grouped[j // 2][:, j % 2, :, :, :]
+            src = x_turned[j][:].bitcast(BF16).rearrange("p u q (m e) -> p q m u e", e=2)
+            for q in range(PASSES):
+                nc.vector.tensor_tensor(
+                    out=dst[:, q, :, :].rearrange("p m (u e) -> p m u e", e=2),
+                    in0=src[:, q],
+                    in1=x_scales[:, q, :].rearrange("p (u e) -> p u e", e=2).unsqueeze(1).to_broadcast([P, P, 2, 2]),
+                    op=MULT,
+                )
+
+        def quantise_x(pair):
+            x_done.add(pair)
+            tiles = slice(2 * pair, 2 * pair + 2)
+            quantise(
+                x_codes[:, tiles, :, :].rearrange("p j q m -> p (j q m)"),
+                x_planes[:, tiles, :, :].rearrange("p j q m -> p (j q m)"),
+                x_grouped[pair][:].rearrange("p j q m t -> p (j q m t)"),
+            )
+
+        blocks = [(h, g, k) for g in range(GROUPS) for h in range(2) for k in range(2)]
+        banks = {}
+        members = {}
+        a_grouped = {}
+        centres = {}
+
+        def chunk_cols(i):
+            h, g, k = blocks[i]
+            return slice(h * HALF + k * CHUNK, h * HALF + (k + 1) * CHUNK)
+
+        def score(i, pair):
+            h, g, k = blocks[i]
+            bank = work.tile([P, 2, CHUNK], F32, name="bank")
+            for s in range(2):
+                j = 4 * g + 2 * pair + s
+                for q in range(PASSES):
+                    nc.tensor.matmul_mx(
+                        out=bank[:, s, :],
+                        lhsT=x_codes[:, j, q, :].bitcast(FP8X4),
+                        lhsT_scale=x_planes[:, j, q, :],
+                        rhs=c_codes[:, q, chunk_cols(i)].bitcast(FP8X4),
+                        rhs_scale=c_planes[:, q, chunk_cols(i)],
+                        start=(q == 0),
+                        stop=(q == PASSES - 1),
+                    )
+            banks[i, pair] = bank
+
+        def unit_slice(i, t0, t1):
+            k = blocks[i][2]
+            return members[i // 2][:, t0:t1, k * CHUNK : (k + 1) * CHUNK]
+
+        def add_bias(i, pair):
+            if i % 2 == 0 and pair == 0:
+                members[i // 2] = zp.tile([P, 4, HALF], F32, name="member")
+            nc.vector.tensor_tensor(
+                out=unit_slice(i, 2 * pair, 2 * pair + 2),
+                in0=banks[i, pair][:],
+                in1=b_all[:, chunk_cols(i)].unsqueeze(1).to_broadcast([P, 2, CHUNK]),
+                op=ADD,
+            )
+
+        def squash(i, pair=None):
+            z = unit_slice(i, 0, 4) if pair is None else unit_slice(i, 2 * pair, 2 * pair + 2)
+            nc.scalar.activation(out=z, in_=z, func=SIGMOID)
+
+        def store_member(i, whole):
+            h, g, k = blocks[i]
+            rows = member_out[g * GROUP : (g + 1) * GROUP, :].rearrange("(p t) n -> p t n", t=4)
+            if whole:
+                nc.sync.dma_start(out=rows[:, :, h * HALF : (h + 1) * HALF], in_=members[i // 2][:])
+            else:
+                nc.sync.dma_start(out=rows[:, :, chunk_cols(i)], in_=unit_slice(i, 0, 4))
+
+        def weigh(i):
+            h, g, k = blocks[i]
+            if i % 2 == 0:
+                a_grouped[i // 2] = agp.tile([P, HALF, 4], BF16, name="a_grouped", align_bytes=64)
+            eng = nc.vector if i in V_BLOCKS else nc.gpsimd
+            width = CHUNK if i in V_BLOCKS else WEIGH_COLS
+            for n in range(k * CHUNK, (k + 1) * CHUNK, width):
+                eng.tensor_tensor(
+                    out=a_grouped[i // 2][:, n : n + width, :],
+                    in0=members[i // 2][:, :, n : n + width].rearrange("p t n -> p n t"),
+                    in1=masses[:, g, :].unsqueeze(1).to_broadcast([P, width, 4]),
+                    op=MULT,
+                )
+
+        def quantise_a(i, whole):
+            h, g, k = blocks[i]
+            if whole:
+                cols = slice(h * HALF, (h + 1) * HALF)
+                part = a_grouped[i // 2][:]
+            else:
+                cols = chunk_cols(i)
+                part = a_grouped[i // 2][:, k * CHUNK : (k + 1) * CHUNK, :]
+            quantise(a_codes[:, g, cols], a_planes[:, g, cols], part.rearrange("p n t -> p (n t)"))
+
+        def centre(h, g, r):
+            if g == 0:
+                centres[h, r] = sums.tile([P, D], F32, name=f"centre{r}") if h == 0 else work.tile([P, D], F32, name="bank")
+            cols = slice(h * HALF + r * P, h * HALF + (r + 1) * P)
+            nc.tensor.matmul_mx(
+                out=centres[h, r][:],
+                lhsT=a_codes[:, g, cols].bitcast(FP8X4),
+                lhsT_scale=a_planes[:, g, cols],
+                rhs=v_codes[:, g, :].bitcast(FP8X4),
+                rhs_scale=v_planes[:, g, :],
+                start=(g == 0),
+                stop=(g == GROUPS - 1),
+            )
+
+        def finish(h, r, eng):
+            result = outp.tile([P, D], F32, name="result")
+            if eng == "s":
+                nc.scalar.copy(out=result[:], in_=centres[h, r][:])
+            else:
+                nc.vector.tensor_copy(out=result[:], in_=centres[h, r][:])
+            nc.sync.dma_start(out=centre_out[h * HALF + r * P : h * HALF + (r + 1) * P, :], in_=result[:])
+
+        def late(i):
+            h, g, k = blocks[i]
+            if i in V_BLOCKS:
+                weigh(i)
+            quantise_a(i, False)
+            for r in range(2 * k, 2 * k + 2):
+                if h == 0:
+                    centre(h, g, r)
+
+        def late_centre(k):
+            for r in range(2 * k, 2 * k + 2):
+                centre(1, GROUPS - 1, r)
+                finish(1, r, FINISH[4 + r])
+
+        with tc.manual_schedule():
+            nc.vector.memset(spark[:], 0.0)
+            nc.scalar.activation(out=spark[:], in_=spark[:], func=SIGMOID)
+            load_x(0, 0, 2)
+            nc.sync.dma_start(out=x_scales[:], in_=x_scale.rearrange("o (q p t) -> p (o q) t", p=P, t=4))
+            load_x(0, 2, 4)
+            load_c(0, 0)
+            load_c(1, 0)
+            nc.vector.memset(b_rows[:], 0.0)
+            nc.vector.memset(ones[:], 1.0)
+            nc.scalar.dma_start(out=b_rows[0:1, :], in_=b.rearrange("(o n) -> o n", o=1))
+            nc.scalar.dma_start(out=masses[:], in_=mass.rearrange("(g p t) -> p g t", p=P, t=4))
+            make_identity(nc, ident[:])
+            load_x(1, 0, 4)
+            load_c(0, 1)
+            load_c(1, 1)
+            load_v(0)
+            load_x(2, 0, 4)
+            load_v(1)
+            load_x(3, 0, 4)
+            load_v(2)
+            load_v(3)
+
+            fills = [("x", j) for j in range(4)] + [("b", h) for h in range(2)]
+            for i in range(16):
+                if i + 4 < 16:
+                    fills.append(("x", i + 4))
+                fills += [("s", i, 0), ("s", i, 1)]
+            pending = list(fills)
+            read = [0]
+
+            def may_fill(what):
+                if len(fills) - len(pending) >= read[0] + 4:
+                    return False
+                if what[0] == "x":
+                    return what[1] in x_wide
+                if what[0] == "s":
+                    h, g, k = blocks[what[1]]
+                    return 2 * g + 1 in x_done and 2 * h + 1 in c_done
+                return True
+
+            def fill():
+                while pending and may_fill(pending[0]):
+                    what = pending[0]
+                    pending.remove(what)
+                    if what[0] == "x":
+                        turn(what[1])
+                    elif what[0] == "b":
+                        spread_b(what[1])
+                    else:
+                        score(what[1], what[2])
+
+            def took():
+                read[0] += 1
+                fill()
+
+            for j in range(4):
+                widen(j)
+                fill()
+            c_grouped = [interleave(C_ENGINES[n], c_raw[n % 2][n // 2]) for n in range(2)]
+            scale_x(0)
+            took()
+            scale_x(1)
+            took()
+            quantise_c(0, 0, c_grouped[0])
+            quantise_x(0)
+            scale_x(2)
+            took()
+            scale_x(3)
+            took()
+            widen(4)
+            c_grouped += [interleave(C_ENGINES[n], c_raw[n % 2][n // 2]) for n in range(2, 4)]
+            for h in range(2):
+                nc.scalar.copy(out=b_all[:, h * HALF : (h + 1) * HALF], in_=b_banks[h][:])
+                took()
+            quantise_c(1, 0, c_grouped[1])
+            quantise_x(1)
+            fill()
+            v_grouped = {0: interleave(V_ENGINES[0], v_raw[0])}
+            widen(5)
+            fill()
+
+            for i in range(len(blocks)):
+                h, g, k = blocks[i]
+                if i + 4 < 16:
+                    scale_x(i + 4)
+                    took()
+                for pair in range(2):
+                    add_bias(i, pair)
+                    took()
+                    if i >= 12:
+                        squash(i, pair)
+                    if pair == 0 and i + 4 < 16 and i % 2 == 1:
+                        quantise_x((i + 4) // 2)
+                        fill()
+                if i < 12:
+                    squash(i)
+                if i + 6 < 16:
+                    widen(i + 6)
+                    fill()
+                if i not in V_BLOCKS:
+                    weigh(i)
+                if i < 2:
+                    quantise_c(i, 1, c_grouped[2 + i])
+                    fill()
+                if i % 4 == 1:
+                    quantise_v(g, v_grouped[g])
+                    if g + 1 < GROUPS:
+                        v_grouped[g + 1] = interleave(V_ENGINES[g + 1], v_raw[g + 1])
+                if i < 12 and k == 1:
+                    store_member(i, True)
+                if i >= 12:
+                    store_member(i, False)
+                if i >= 3 and i < 14 and i % 2 == 1:
+                    quantise_a(i - 2, True)
+                if i >= 4 and i % 2 == 0 and blocks[i - 3][0] == 0:
+                    for r in range(4):
+                        centre(0, blocks[i - 3][1], r)
+                if i >= 13:
+                    late(i - 1)
+            for r in range(4):
+                finish(0, r, FINISH[r])
+                for g in range(GROUPS - 1):
+                    centre(1, g, r)
+            late_centre(0)
+            late(15)
+            late_centre(1)

@@ -75,13 +75,14 @@ def tile_soft_cluster_centres_s7_kernel(tc, x_bytes, x_scale, c, b, mass, v, mem
 
         def interleave(eng, raw):
             grouped = cvp.tile([P, 512, 4], BF16, name="cv_grouped", align_bytes=64)
-            src = raw[:].rearrange("p t n -> p n t")
+            src = raw[:].rearrange("p t (n i) -> p n t i", i=4)
+            dst = grouped[:].rearrange("p (n i) t -> p n t i", i=4)
             if eng == "v":
-                nc.vector.tensor_copy(out=grouped[:], in_=src)
+                nc.vector.tensor_copy(out=dst, in_=src)
             elif eng == "s":
-                nc.scalar.copy(out=grouped[:], in_=src)
+                nc.scalar.copy(out=dst, in_=src)
             else:
-                nc.gpsimd.tensor_scalar(out=grouped[:], in0=src, scalar1=1.0, scalar2=0.0, op0=MULT, op1=ADD)
+                nc.gpsimd.tensor_scalar(out=dst, in0=src, scalar1=1.0, scalar2=0.0, op0=MULT, op1=ADD)
             return grouped
 
         def quantise(codes, planes, grouped):
@@ -204,9 +205,9 @@ def tile_soft_cluster_centres_s7_kernel(tc, x_bytes, x_scale, c, b, mass, v, mem
             width = CHUNK if i in V_BLOCKS else WEIGH_COLS
             for n in range(k * CHUNK, (k + 1) * CHUNK, width):
                 eng.tensor_tensor(
-                    out=a_grouped[i // 2][:, n : n + width, :],
-                    in0=members[i // 2][:, :, n : n + width].rearrange("p t n -> p n t"),
-                    in1=masses[:, g, :].unsqueeze(1).to_broadcast([P, width, 4]),
+                    out=a_grouped[i // 2][:, n : n + width, :].rearrange("p (n i) t -> p n t i", i=4),
+                    in0=members[i // 2][:, :, n : n + width].rearrange("p t (n i) -> p n t i", i=4),
+                    in1=masses[:, g, :].unsqueeze(1).unsqueeze(3).to_broadcast([P, width // 4, 4, 4]),
                     op=MULT,
                 )
 
@@ -343,6 +344,9 @@ def tile_soft_cluster_centres_s7_kernel(tc, x_bytes, x_scale, c, b, mass, v, mem
                 if i + 4 < 16:
                     scale_x(i + 4)
                     took()
+                if i + 6 < 16:
+                    widen(i + 6)
+                    fill()
                 for pair in range(2):
                     add_bias(i, pair)
                     took()
@@ -353,9 +357,6 @@ def tile_soft_cluster_centres_s7_kernel(tc, x_bytes, x_scale, c, b, mass, v, mem
                         fill()
                 if i < 12:
                     squash(i)
-                if i + 6 < 16:
-                    widen(i + 6)
-                    fill()
                 if i not in V_BLOCKS:
                     weigh(i)
                 if i < 2:

@@ -23,10 +23,12 @@ GROUPS = M // GROUP
 PASSES = K // 512
 HALF = 512
 CHUNK = 256
-V_BLOCKS = (12, 13, 14, 15)
-C_ENGINES = ("g", "s", "g", "s")
+KINDS = "ttttttttttvvvvvv"
+X_STEPS = [[5], [6], [7], [8], [9], [10], [11], [12, 13], [14, 15]] + [[]] * 7
+IL_COLS = 128
+C_ENGINES = ("v", "s", "s", "s")
 WEIGH_COLS = 64
-V_ENGINES = ("s", "s", "s", "s")
+V_ENGINES = ("g", "g", "g", "g")
 FINISH = ("s", "s", "s", "s", "s", "s", "s", "v")
 
 
@@ -39,6 +41,7 @@ def tile_soft_cluster_centres_s7_kernel(tc, x_bytes, x_scale, c, b, mass, v, mem
         cvp = ctx.enter_context(tc.tile_pool(name="cvp", bufs=6))
         agp = ctx.enter_context(tc.tile_pool(name="agp", bufs=3))
         zp = ctx.enter_context(tc.tile_pool(name="zp", bufs=4))
+        flip = ctx.enter_context(tc.tile_pool(name="flip", bufs=6))
         outp = ctx.enter_context(tc.tile_pool(name="outp", bufs=8))
         work = ctx.enter_context(tc.psum_pool(name="work", bufs=4))
         sums = ctx.enter_context(tc.psum_pool(name="sums", bufs=1))
@@ -46,8 +49,8 @@ def tile_soft_cluster_centres_s7_kernel(tc, x_bytes, x_scale, c, b, mass, v, mem
         x_raw = [keep.tile([P, 4, K], U8, name=f"x_raw{g}", align_bytes=64) for g in range(GROUPS)]
         c_raw = [[keep.tile([P, 4, HALF], BF16, name=f"c_raw{q}{h}", align_bytes=64) for h in range(2)] for q in range(PASSES)]
         v_raw = [keep.tile([P, 4, D], BF16, name=f"v_raw{g}", align_bytes=64) for g in range(GROUPS)]
-        x_codes = keep.tile([P, 4 * GROUPS, PASSES, P], U32, name="x_codes", align_bytes=64)
-        x_planes = keep.tile([P, 4 * GROUPS, PASSES, P], U8, name="x_planes", align_bytes=64)
+        x_codes = keep.tile([P, GROUPS, PASSES, 4, P], U32, name="x_codes", align_bytes=64)
+        x_planes = keep.tile([P, GROUPS, PASSES, 4, P], U8, name="x_planes", align_bytes=64)
         c_codes = keep.tile([P, PASSES, R], U32, name="c_codes", align_bytes=64)
         c_planes = keep.tile([P, PASSES, R], U8, name="c_planes", align_bytes=64)
         v_codes = keep.tile([P, GROUPS, D], U32, name="v_codes", align_bytes=64)
@@ -56,9 +59,10 @@ def tile_soft_cluster_centres_s7_kernel(tc, x_bytes, x_scale, c, b, mass, v, mem
         a_planes = keep.tile([P, GROUPS, R], U8, name="a_planes", align_bytes=64)
         x_scales = keep.tile([P, PASSES, 4], F32, name="x_scales")
         masses = keep.tile([P, GROUPS, 4], BF16, name="masses")
-        b_rows = keep.tile([P, R], BF16, name="b_rows")
-        b_all = keep.tile([P, R], F32, name="b_all")
-        ones = keep.tile([P, P], BF16, name="ones")
+        b_all = keep.tile([P, R], BF16, name="b_all")
+        b_cols = keep.tile([P, 8], F32, name="b_cols")
+        b_eight = keep.tile([P, P], BF16, name="b_eight")
+        ident_bf = keep.tile([P, P], BF16, name="ident_bf")
         ident = keep.tile([P, P], F32, name="ident")
         spark = keep.tile([P, 1], F32, name="spark")
 
@@ -75,14 +79,16 @@ def tile_soft_cluster_centres_s7_kernel(tc, x_bytes, x_scale, c, b, mass, v, mem
 
         def interleave(eng, raw):
             grouped = cvp.tile([P, 512, 4], BF16, name="cv_grouped", align_bytes=64)
-            src = raw[:].rearrange("p t (n i) -> p n t i", i=4)
-            dst = grouped[:].rearrange("p (n i) t -> p n t i", i=4)
-            if eng == "v":
-                nc.vector.tensor_copy(out=dst, in_=src)
-            elif eng == "s":
-                nc.scalar.copy(out=dst, in_=src)
-            else:
-                nc.gpsimd.tensor_scalar(out=dst, in0=src, scalar1=1.0, scalar2=0.0, op0=MULT, op1=ADD)
+            width = IL_COLS if eng == "g" else 512
+            for n in range(0, 512, width):
+                src = raw[:, :, n : n + width].rearrange("p t (n i) -> p n t i", i=4)
+                dst = grouped[:, n : n + width, :].rearrange("p (n i) t -> p n t i", i=4)
+                if eng == "v":
+                    nc.vector.tensor_copy(out=dst, in_=src)
+                elif eng == "s":
+                    nc.scalar.copy(out=dst, in_=src)
+                else:
+                    nc.gpsimd.tensor_scalar(out=dst, in0=src, scalar1=1.0, scalar2=0.0, op0=MULT, op1=ADD)
             return grouped
 
         def quantise(codes, planes, grouped):
@@ -100,6 +106,7 @@ def tile_soft_cluster_centres_s7_kernel(tc, x_bytes, x_scale, c, b, mass, v, mem
         x_turned = {}
         x_grouped = {}
         x_done = set()
+        taken = set()
         c_done = set()
 
         def widen(j):
@@ -116,35 +123,36 @@ def tile_soft_cluster_centres_s7_kernel(tc, x_bytes, x_scale, c, b, mass, v, mem
                     nc.tensor.transpose(bank[:, u, q, :], words[:, q * 256 + u : (q + 1) * 256 : 2], ident[:])
             x_turned[j] = bank
 
-        b_banks = {}
-
-        def spread_b(h):
-            b_banks[h] = work.tile([P, HALF], F32, name="bank")
-            nc.tensor.matmul(out=b_banks[h][:], lhsT=ones[:], rhs=b_rows[:, h * HALF : (h + 1) * HALF], start=True, stop=True)
+        def spread_b():
+            bank = work.tile([P, P], F32, name="bank")
+            nc.tensor.matmul(out=bank[:], lhsT=b_eight[:], rhs=ident_bf[:], start=True, stop=True)
+            nc.scalar.copy(out=b_cols[:], in_=bank[:, 0:8])
+            taken.add(("b",))
 
         def scale_x(j):
-            if j % 2 == 0:
-                x_grouped[j // 2] = xgp.tile([P, 2, PASSES, P, 4], BF16, name="x_grouped", align_bytes=64)
-            dst = x_grouped[j // 2][:, j % 2, :, :, :]
+            g, t = j // 4, j % 4
+            if t == 0:
+                x_grouped[g] = xgp.tile([P, PASSES, 4, P, 4], BF16, name="x_grouped", align_bytes=64)
             src = x_turned[j][:].bitcast(BF16).rearrange("p u q (m e) -> p q m u e", e=2)
             for q in range(PASSES):
                 nc.vector.tensor_tensor(
-                    out=dst[:, q, :, :].rearrange("p m (u e) -> p m u e", e=2),
+                    out=x_grouped[g][:, q, t, :, :].rearrange("p m (u e) -> p m u e", e=2),
                     in0=src[:, q],
                     in1=x_scales[:, q, :].rearrange("p (u e) -> p u e", e=2).unsqueeze(1).to_broadcast([P, P, 2, 2]),
                     op=MULT,
                 )
 
-        def quantise_x(pair):
-            x_done.add(pair)
-            tiles = slice(2 * pair, 2 * pair + 2)
+        def quantise_x(g, q, t0, t1):
             quantise(
-                x_codes[:, tiles, :, :].rearrange("p j q m -> p (j q m)"),
-                x_planes[:, tiles, :, :].rearrange("p j q m -> p (j q m)"),
-                x_grouped[pair][:].rearrange("p j q m t -> p (j q m t)"),
+                x_codes[:, g, q, t0:t1, :].rearrange("p t m -> p (t m)"),
+                x_planes[:, g, q, t0:t1, :].rearrange("p t m -> p (t m)"),
+                x_grouped[g][:, q, t0:t1, :, :].rearrange("p t m k -> p (t m k)"),
             )
+            if t1 == 4 and q == PASSES - 1:
+                x_done.add(g)
 
-        blocks = [(h, g, k) for g in range(GROUPS) for h in range(2) for k in range(2)]
+        units = [(0, 0), (1, 0), (0, 1), (1, 1), (0, 2), (0, 3), (1, 2), (1, 3)]
+        blocks = [(h, g, k) for h, g in units for k in range(2)]
         banks = {}
         members = {}
         a_grouped = {}
@@ -156,28 +164,83 @@ def tile_soft_cluster_centres_s7_kernel(tc, x_bytes, x_scale, c, b, mass, v, mem
 
         def score(i, pair):
             h, g, k = blocks[i]
-            bank = work.tile([P, 2, CHUNK], F32, name="bank")
-            for s in range(2):
-                j = 4 * g + 2 * pair + s
+            if KINDS[i] == "t":
+                bank = work.tile([P, 4 * P], F32, name="bank")
+                cols = slice(h * HALF + k * CHUNK + pair * P, h * HALF + k * CHUNK + (pair + 1) * P)
                 for q in range(PASSES):
                     nc.tensor.matmul_mx(
-                        out=bank[:, s, :],
-                        lhsT=x_codes[:, j, q, :].bitcast(FP8X4),
-                        lhsT_scale=x_planes[:, j, q, :],
-                        rhs=c_codes[:, q, chunk_cols(i)].bitcast(FP8X4),
-                        rhs_scale=c_planes[:, q, chunk_cols(i)],
+                        out=bank[:],
+                        lhsT=c_codes[:, q, cols].bitcast(FP8X4),
+                        lhsT_scale=c_planes[:, q, cols],
+                        rhs=x_codes[:, g, q, :, :].rearrange("p t m -> p (t m)").bitcast(FP8X4),
+                        rhs_scale=x_planes[:, g, q, :, :].rearrange("p t m -> p (t m)"),
                         start=(q == 0),
                         stop=(q == PASSES - 1),
                     )
+            else:
+                bank = work.tile([P, 2, CHUNK], F32, name="bank")
+                for s in range(2):
+                    for q in range(PASSES):
+                        nc.tensor.matmul_mx(
+                            out=bank[:, s, :],
+                            lhsT=x_codes[:, g, q, 2 * pair + s, :].bitcast(FP8X4),
+                            lhsT_scale=x_planes[:, g, q, 2 * pair + s, :],
+                            rhs=c_codes[:, q, chunk_cols(i)].bitcast(FP8X4),
+                            rhs_scale=c_planes[:, q, chunk_cols(i)],
+                            start=(q == 0),
+                            stop=(q == PASSES - 1),
+                        )
             banks[i, pair] = bank
+
+        flipped = {}
+        returned = {}
+
+        def squash_flipped(i, pair):
+            h, g, k = blocks[i]
+            r = 4 * h + 2 * k + pair
+            flipped[i, pair] = flip.tile([P, 4 * P], F32, name="flipped")
+            nc.scalar.activation(out=flipped[i, pair][:], in_=banks[i, pair][:], func=SIGMOID, bias=b_cols[:, r : r + 1])
+
+        def turn_back(i, pair):
+            bank = work.tile([P, 4, P], F32, name="bank")
+            for t in range(4):
+                nc.tensor.transpose(bank[:, t, :], flipped[i, pair][:, t * P : (t + 1) * P], ident[:])
+            returned[i, pair] = bank
+
+        def member_tile(i):
+            if i // 2 not in members:
+                members[i // 2] = zp.tile([P, 4, HALF], F32, name="member")
+            return members[i // 2]
+
+        def a_tile(i):
+            if i // 2 not in a_grouped:
+                a_grouped[i // 2] = agp.tile([P, HALF, 4], BF16, name="a_grouped", align_bytes=64)
+            return a_grouped[i // 2]
+
+        def keep_member(i, pair, eng):
+            k = blocks[i][2]
+            cols = slice(k * CHUNK + pair * P, k * CHUNK + (pair + 1) * P)
+            if eng == "s":
+                nc.scalar.copy(out=member_tile(i)[:, :, cols], in_=returned[i, pair][:])
+            else:
+                nc.vector.tensor_copy(out=member_tile(i)[:, :, cols], in_=returned[i, pair][:])
+
+        def weigh_returned(i, pair):
+            h, g, k = blocks[i]
+            n = k * CHUNK + pair * P
+            nc.vector.tensor_tensor(
+                out=a_tile(i)[:, n : n + P, :],
+                in0=returned[i, pair][:].rearrange("p t n -> p n t"),
+                in1=masses[:, g, :].unsqueeze(1).to_broadcast([P, P, 4]),
+                op=MULT,
+            )
 
         def unit_slice(i, t0, t1):
             k = blocks[i][2]
             return members[i // 2][:, t0:t1, k * CHUNK : (k + 1) * CHUNK]
 
         def add_bias(i, pair):
-            if i % 2 == 0 and pair == 0:
-                members[i // 2] = zp.tile([P, 4, HALF], F32, name="member")
+            member_tile(i)
             nc.vector.tensor_tensor(
                 out=unit_slice(i, 2 * pair, 2 * pair + 2),
                 in0=banks[i, pair][:],
@@ -199,10 +262,9 @@ def tile_soft_cluster_centres_s7_kernel(tc, x_bytes, x_scale, c, b, mass, v, mem
 
         def weigh(i):
             h, g, k = blocks[i]
-            if i % 2 == 0:
-                a_grouped[i // 2] = agp.tile([P, HALF, 4], BF16, name="a_grouped", align_bytes=64)
-            eng = nc.vector if i in V_BLOCKS else nc.gpsimd
-            width = CHUNK if i in V_BLOCKS else WEIGH_COLS
+            a_tile(i)
+            eng = nc.vector if KINDS[i] == "v" else nc.gpsimd
+            width = CHUNK if KINDS[i] == "v" else WEIGH_COLS
             for n in range(k * CHUNK, (k + 1) * CHUNK, width):
                 eng.tensor_tensor(
                     out=a_grouped[i // 2][:, n : n + width, :].rearrange("p (n i) t -> p n t i", i=4),
@@ -223,7 +285,7 @@ def tile_soft_cluster_centres_s7_kernel(tc, x_bytes, x_scale, c, b, mass, v, mem
 
         def centre(h, g, r):
             if g == 0:
-                centres[h, r] = sums.tile([P, D], F32, name=f"centre{r}") if h == 0 else work.tile([P, D], F32, name="bank")
+                centres[h, r] = sums.tile([P, D], F32, name=f"centre{r}")
             cols = slice(h * HALF + r * P, h * HALF + (r + 1) * P)
             nc.tensor.matmul_mx(
                 out=centres[h, r][:],
@@ -243,20 +305,6 @@ def tile_soft_cluster_centres_s7_kernel(tc, x_bytes, x_scale, c, b, mass, v, mem
                 nc.vector.tensor_copy(out=result[:], in_=centres[h, r][:])
             nc.sync.dma_start(out=centre_out[h * HALF + r * P : h * HALF + (r + 1) * P, :], in_=result[:])
 
-        def late(i):
-            h, g, k = blocks[i]
-            if i in V_BLOCKS:
-                weigh(i)
-            quantise_a(i, False)
-            for r in range(2 * k, 2 * k + 2):
-                if h == 0:
-                    centre(h, g, r)
-
-        def late_centre(k):
-            for r in range(2 * k, 2 * k + 2):
-                centre(1, GROUPS - 1, r)
-                finish(1, r, FINISH[4 + r])
-
         with tc.manual_schedule():
             nc.vector.memset(spark[:], 0.0)
             nc.scalar.activation(out=spark[:], in_=spark[:], func=SIGMOID)
@@ -265,11 +313,11 @@ def tile_soft_cluster_centres_s7_kernel(tc, x_bytes, x_scale, c, b, mass, v, mem
             load_x(0, 2, 4)
             load_c(0, 0)
             load_c(1, 0)
-            nc.vector.memset(b_rows[:], 0.0)
-            nc.vector.memset(ones[:], 1.0)
-            nc.scalar.dma_start(out=b_rows[0:1, :], in_=b.rearrange("(o n) -> o n", o=1))
+            nc.vector.memset(b_eight[:], 0.0)
+            nc.scalar.dma_start(out=b_eight[0:8, :], in_=b.rearrange("(r p) -> r p", p=P))
             nc.scalar.dma_start(out=masses[:], in_=mass.rearrange("(g p t) -> p g t", p=P, t=4))
             make_identity(nc, ident[:])
+            nc.gpsimd.tensor_copy(out=ident_bf[:], in_=ident[:])
             load_x(1, 0, 4)
             load_c(0, 1)
             load_c(1, 1)
@@ -279,23 +327,29 @@ def tile_soft_cluster_centres_s7_kernel(tc, x_bytes, x_scale, c, b, mass, v, mem
             load_x(3, 0, 4)
             load_v(2)
             load_v(3)
+            nc.sync.dma_start(out=b_all[:], in_=b.partition_broadcast(P))
 
-            fills = [("x", j) for j in range(4)] + [("b", h) for h in range(2)]
+            fills = [("x", j) for j in range(4)] + [("b",)] + [("x", 4)]
+            fills += [("s", 0, 0), ("s", 0, 1)]
             for i in range(16):
-                if i + 4 < 16:
-                    fills.append(("x", i + 4))
-                fills += [("s", i, 0), ("s", i, 1)]
+                fills += [("x", j) for j in X_STEPS[i]]
+                if KINDS[i] == "t":
+                    fills += [("r", i, 0), ("r", i, 1)]
+                if i + 1 < 16:
+                    fills += [("s", i + 1, 0), ("s", i + 1, 1)]
             pending = list(fills)
-            read = [0]
 
             def may_fill(what):
-                if len(fills) - len(pending) >= read[0] + 4:
+                n = len(fills) - len(pending)
+                if n >= 4 and fills[n - 4] not in taken:
                     return False
                 if what[0] == "x":
                     return what[1] in x_wide
                 if what[0] == "s":
                     h, g, k = blocks[what[1]]
-                    return 2 * g + 1 in x_done and 2 * h + 1 in c_done
+                    return g in x_done and 2 * h + 1 in c_done
+                if what[0] == "r":
+                    return (what[1], what[2]) in flipped
                 return True
 
             def fill():
@@ -305,82 +359,121 @@ def tile_soft_cluster_centres_s7_kernel(tc, x_bytes, x_scale, c, b, mass, v, mem
                     if what[0] == "x":
                         turn(what[1])
                     elif what[0] == "b":
-                        spread_b(what[1])
-                    else:
+                        spread_b()
+                    elif what[0] == "s":
                         score(what[1], what[2])
+                    else:
+                        turn_back(what[1], what[2])
 
-            def took():
-                read[0] += 1
+            def took(*what):
+                taken.add(what)
                 fill()
+
+            def take_x(j):
+                scale_x(j)
+                took("x", j)
+
+            x_ahead = [j for js in X_STEPS for j in js]
+
+            def widen_next():
+                if x_ahead:
+                    widen(x_ahead[0])
+                    x_ahead.remove(x_ahead[0])
+                    fill()
 
             for j in range(4):
                 widen(j)
                 fill()
+            take_x(0)
+            take_x(1)
             c_grouped = [interleave(C_ENGINES[n], c_raw[n % 2][n // 2]) for n in range(2)]
-            scale_x(0)
-            took()
-            scale_x(1)
-            took()
+            take_x(2)
             quantise_c(0, 0, c_grouped[0])
-            quantise_x(0)
-            scale_x(2)
-            took()
-            scale_x(3)
-            took()
+            take_x(3)
             widen(4)
-            c_grouped += [interleave(C_ENGINES[n], c_raw[n % 2][n // 2]) for n in range(2, 4)]
-            for h in range(2):
-                nc.scalar.copy(out=b_all[:, h * HALF : (h + 1) * HALF], in_=b_banks[h][:])
-                took()
+            widen_next()
+            c_grouped.append(interleave(C_ENGINES[2], c_raw[0][1]))
+            quantise_x(0, 0, 0, 4)
             quantise_c(1, 0, c_grouped[1])
-            quantise_x(1)
+            quantise_x(0, 1, 0, 4)
             fill()
+            take_x(4)
+            widen_next()
             v_grouped = {0: interleave(V_ENGINES[0], v_raw[0])}
-            widen(5)
-            fill()
+            if KINDS[0] == "t":
+                for pair in range(2):
+                    squash_flipped(0, pair)
+                    took("s", 0, pair)
+            c_grouped.append(interleave(C_ENGINES[3], c_raw[1][1]))
 
             for i in range(len(blocks)):
                 h, g, k = blocks[i]
-                if i + 4 < 16:
-                    scale_x(i + 4)
-                    took()
-                if i + 6 < 16:
-                    widen(i + 6)
-                    fill()
-                for pair in range(2):
-                    add_bias(i, pair)
-                    took()
-                    if i >= 12:
-                        squash(i, pair)
-                    if pair == 0 and i + 4 < 16 and i % 2 == 1:
-                        quantise_x((i + 4) // 2)
+                kind = KINDS[i]
+                for j in X_STEPS[i]:
+                    take_x(j)
+                    if j % 4 == 3:
+                        for q in range(PASSES):
+                            quantise_x(j // 4, q, 0, 4)
                         fill()
-                if i < 12:
-                    squash(i)
-                if i not in V_BLOCKS:
-                    weigh(i)
-                if i < 2:
-                    quantise_c(i, 1, c_grouped[2 + i])
+                    widen_next()
+                if kind == "t":
+                    weigh_returned(i, 0)
+                    keep_member(i, 1, "s")
+                    keep_member(i, 0, "s")
+                    took("r", i, 0)
+                    weigh_returned(i, 1)
+                    took("r", i, 1)
+                else:
+                    if i + 1 < 16 and KINDS[i + 1] == "t" and not X_STEPS[i]:
+                        for pair in range(2):
+                            squash_flipped(i + 1, pair)
+                            took("s", i + 1, pair)
+                    for pair in range(2):
+                        add_bias(i, pair)
+                        took("s", i, pair)
+                        squash(i, pair)
+                if i == 0:
+                    quantise_c(0, 1, c_grouped[2])
+                    quantise_c(1, 1, c_grouped[3])
                     fill()
-                if i % 4 == 1:
-                    quantise_v(g, v_grouped[g])
-                    if g + 1 < GROUPS:
-                        v_grouped[g + 1] = interleave(V_ENGINES[g + 1], v_raw[g + 1])
-                if i < 12 and k == 1:
+                if i + 1 < 16 and KINDS[i + 1] == "t" and (kind == "t" or X_STEPS[i]):
+                    for pair in range(2):
+                        squash_flipped(i + 1, pair)
+                        took("s", i + 1, pair)
+                if i >= 1 and KINDS[i - 1] == "v":
+                    weigh(i - 1)
+                if i in (1, 3, 5, 7):
+                    n = i // 2
+                    quantise_v(n, v_grouped[n])
+                    if n + 1 < GROUPS:
+                        v_grouped[n + 1] = interleave(V_ENGINES[n + 1], v_raw[n + 1])
+                if i < 14 and k == 1:
                     store_member(i, True)
-                if i >= 12:
+                if i >= 14:
                     store_member(i, False)
-                if i >= 3 and i < 14 and i % 2 == 1:
-                    quantise_a(i - 2, True)
-                if i >= 4 and i % 2 == 0 and blocks[i - 3][0] == 0:
+                u = i // 2 - 1
+                if i >= 2 and i % 2 == 0:
+                    quantise_a(2 * u, True)
+                if i >= 3 and i % 2 == 1:
+                    if units[u][0] == 0:
+                        for r in range(4):
+                            centre(0, units[u][1], r)
+                            if u == 5:
+                                finish(0, r, FINISH[r])
+                if i == 14:
+                    for g2 in range(2):
+                        for r in range(4):
+                            centre(1, g2, r)
+                if i == 15:
                     for r in range(4):
-                        centre(0, blocks[i - 3][1], r)
-                if i >= 13:
-                    late(i - 1)
-            for r in range(4):
-                finish(0, r, FINISH[r])
-                for g in range(GROUPS - 1):
-                    centre(1, g, r)
-            late_centre(0)
-            late(15)
-            late_centre(1)
+                        centre(1, 2, r)
+                    quantise_a(14, False)
+                    for r in range(2):
+                        centre(1, GROUPS - 1, r)
+                        finish(1, r, FINISH[4 + r])
+            if KINDS[15] == "v":
+                weigh(15)
+            quantise_a(15, False)
+            for r in range(2, 4):
+                centre(1, GROUPS - 1, r)
+                finish(1, r, FINISH[4 + r])

@@ -15,7 +15,6 @@ FP8X4 = mybir.dt.float8_e4m3fn_x4
 MULT = mybir.AluOpType.mult
 ADD = mybir.AluOpType.add
 SIGMOID = mybir.ActivationFunctionType.Sigmoid
-COPY = mybir.ActivationFunctionType.Copy
 
 P = 128
 GROUP = 512
@@ -23,36 +22,39 @@ GROUPS = M // GROUP
 PASSES = K // 512
 HALF = 512
 CHUNK = 256
-KINDS = "ttttttttttvvvvvv"
-X_STEPS = [[5], [6], [7], [8], [9], [10], [11], [12, 13], [14, 15]] + [[]] * 7
-IL_COLS = 128
-C_ENGINES = ("v", "s", "s", "s")
-WEIGH_COLS = 64
-V_ENGINES = ("g", "g", "g", "g")
-FINISH = ("s", "s", "s", "s", "s", "s", "s", "v")
+KINDS = "gggggggggggvgvgv"
+WEIGH_COLS = 128
+IL_COLS = 512
+C_ENGINES = ("v", "g", "s", "g")
+V_ENGINES = ("s", "s", "s", "s")
+UNITS = ((0, 0), (1, 0), (0, 1), (1, 1), (0, 2), (0, 3), (1, 2), (1, 3))
+X_STEPS = ((5,), (6,), (7,), (8,), (9,), (10,), (11,), (12, 13), (14, 15)) + ((),) * 7
+V_STEPS = (3, 7, 8, 9)
+H0_STEPS = {13: (0,), 14: (1,), 15: (2, 3)}
+BANKS = 8
+FINISH = "ssssssvs"
+A_UNIT = (-1, -1, -1, -1, 0, -1, 1, -1, 2, -1, 3, -1, 4, 5, -1, 6)
 
 
 def tile_soft_cluster_centres_s7_kernel(tc, x_bytes, x_scale, c, b, mass, v, member_out, centre_out):
     nc = tc.nc
     with ExitStack() as ctx:
         keep = ctx.enter_context(tc.tile_pool(name="keep", bufs=1))
-        wide = ctx.enter_context(tc.tile_pool(name="wide", bufs=4))
+        wide = ctx.enter_context(tc.tile_pool(name="wide", bufs=6))
         xgp = ctx.enter_context(tc.tile_pool(name="xgp", bufs=2))
         cvp = ctx.enter_context(tc.tile_pool(name="cvp", bufs=6))
         agp = ctx.enter_context(tc.tile_pool(name="agp", bufs=3))
-        zp = ctx.enter_context(tc.tile_pool(name="zp", bufs=4))
-        flip = ctx.enter_context(tc.tile_pool(name="flip", bufs=6))
+        zp = ctx.enter_context(tc.tile_pool(name="zp", bufs=5))
         outp = ctx.enter_context(tc.tile_pool(name="outp", bufs=8))
-        work = ctx.enter_context(tc.psum_pool(name="work", bufs=4))
-        sums = ctx.enter_context(tc.psum_pool(name="sums", bufs=1))
+        psum = ctx.enter_context(tc.psum_pool(name="psum", bufs=BANKS))
 
         x_raw = [keep.tile([P, 4, K], U8, name=f"x_raw{g}", align_bytes=64) for g in range(GROUPS)]
         c_raw = [[keep.tile([P, 4, HALF], BF16, name=f"c_raw{q}{h}", align_bytes=64) for h in range(2)] for q in range(PASSES)]
         v_raw = [keep.tile([P, 4, D], BF16, name=f"v_raw{g}", align_bytes=64) for g in range(GROUPS)]
-        x_codes = keep.tile([P, GROUPS, PASSES, 4, P], U32, name="x_codes", align_bytes=64)
-        x_planes = keep.tile([P, GROUPS, PASSES, 4, P], U8, name="x_planes", align_bytes=64)
-        c_codes = keep.tile([P, PASSES, R], U32, name="c_codes", align_bytes=64)
-        c_planes = keep.tile([P, PASSES, R], U8, name="c_planes", align_bytes=64)
+        x_codes = keep.tile([P, 4 * GROUPS, PASSES, P], U32, name="x_codes", align_bytes=64)
+        x_planes = keep.tile([P, 4 * GROUPS, PASSES, P], U8, name="x_planes", align_bytes=64)
+        c_codes = keep.tile([P, 2, PASSES, HALF], U32, name="c_codes", align_bytes=64)
+        c_planes = keep.tile([P, 2, PASSES, HALF], U8, name="c_planes", align_bytes=64)
         v_codes = keep.tile([P, GROUPS, D], U32, name="v_codes", align_bytes=64)
         v_planes = keep.tile([P, GROUPS, D], U8, name="v_planes", align_bytes=64)
         a_codes = keep.tile([P, GROUPS, R], U32, name="a_codes", align_bytes=64)
@@ -60,9 +62,6 @@ def tile_soft_cluster_centres_s7_kernel(tc, x_bytes, x_scale, c, b, mass, v, mem
         x_scales = keep.tile([P, PASSES, 4], F32, name="x_scales")
         masses = keep.tile([P, GROUPS, 4], BF16, name="masses")
         b_all = keep.tile([P, R], BF16, name="b_all")
-        b_cols = keep.tile([P, 8], F32, name="b_cols")
-        b_eight = keep.tile([P, P], BF16, name="b_eight")
-        ident_bf = keep.tile([P, P], BF16, name="ident_bf")
         ident = keep.tile([P, P], F32, name="ident")
         spark = keep.tile([P, 1], F32, name="spark")
 
@@ -81,8 +80,12 @@ def tile_soft_cluster_centres_s7_kernel(tc, x_bytes, x_scale, c, b, mass, v, mem
             grouped = cvp.tile([P, 512, 4], BF16, name="cv_grouped", align_bytes=64)
             width = IL_COLS if eng == "g" else 512
             for n in range(0, 512, width):
-                src = raw[:, :, n : n + width].rearrange("p t (n i) -> p n t i", i=4)
-                dst = grouped[:, n : n + width, :].rearrange("p (n i) t -> p n t i", i=4)
+                if eng == "g":
+                    src = raw[:, :, n : n + width].rearrange("p t n -> p n t")
+                    dst = grouped[:, n : n + width, :]
+                else:
+                    src = raw[:, :, n : n + width].rearrange("p t (n i) -> p n t i", i=4)
+                    dst = grouped[:, n : n + width, :].rearrange("p (n i) t -> p n t i", i=4)
                 if eng == "v":
                     nc.vector.tensor_copy(out=dst, in_=src)
                 elif eng == "s":
@@ -95,9 +98,7 @@ def tile_soft_cluster_centres_s7_kernel(tc, x_bytes, x_scale, c, b, mass, v, mem
             nc.vector.quantize_mx(out=codes.bitcast(FP8X4), scales=planes, in_=grouped)
 
         def quantise_c(q, h, grouped):
-            c_done.add(2 * h + q)
-            cols = slice(h * HALF, (h + 1) * HALF)
-            quantise(c_codes[:, q, cols], c_planes[:, q, cols], grouped[:].rearrange("p n t -> p (n t)"))
+            quantise(c_codes[:, h, q, :], c_planes[:, h, q, :], grouped[:].rearrange("p n t -> p (n t)"))
 
         def quantise_v(g, grouped):
             quantise(v_codes[:, g, :], v_planes[:, g, :], grouped[:].rearrange("p n t -> p (n t)"))
@@ -105,54 +106,41 @@ def tile_soft_cluster_centres_s7_kernel(tc, x_bytes, x_scale, c, b, mass, v, mem
         x_wide = {}
         x_turned = {}
         x_grouped = {}
-        x_done = set()
-        taken = set()
-        c_done = set()
 
         def widen(j):
             g, t = j // 4, j % 4
-            w = wide.tile([P, K], BF16, name="x_wide")
-            nc.scalar.activation(out=w[:], in_=x_raw[g][:, t, :].bitcast(FP8), func=COPY)
-            x_wide[j] = w
+            x_wide[j] = wide.tile([P, K], BF16, name="x_wide")
+            nc.scalar.copy(out=x_wide[j][:], in_=x_raw[g][:, t, :].bitcast(FP8))
 
         def turn(j):
             words = x_wide[j][:].bitcast(F32)
-            bank = work.tile([P, 2, PASSES, P], F32, name="bank")
+            bank = psum.tile([P, 2, PASSES, P], F32, name="bank")
             for u in range(2):
                 for q in range(PASSES):
                     nc.tensor.transpose(bank[:, u, q, :], words[:, q * 256 + u : (q + 1) * 256 : 2], ident[:])
             x_turned[j] = bank
 
-        def spread_b():
-            bank = work.tile([P, P], F32, name="bank")
-            nc.tensor.matmul(out=bank[:], lhsT=b_eight[:], rhs=ident_bf[:], start=True, stop=True)
-            nc.scalar.copy(out=b_cols[:], in_=bank[:, 0:8])
-            taken.add(("b",))
-
         def scale_x(j):
-            g, t = j // 4, j % 4
-            if t == 0:
-                x_grouped[g] = xgp.tile([P, PASSES, 4, P, 4], BF16, name="x_grouped", align_bytes=64)
+            if j % 4 == 0:
+                x_grouped[j // 4] = xgp.tile([P, 4, PASSES, P, 4], BF16, name="x_grouped", align_bytes=64)
             src = x_turned[j][:].bitcast(BF16).rearrange("p u q (m e) -> p q m u e", e=2)
-            for q in range(PASSES):
-                nc.vector.tensor_tensor(
-                    out=x_grouped[g][:, q, t, :, :].rearrange("p m (u e) -> p m u e", e=2),
-                    in0=src[:, q],
-                    in1=x_scales[:, q, :].rearrange("p (u e) -> p u e", e=2).unsqueeze(1).to_broadcast([P, P, 2, 2]),
-                    op=MULT,
-                )
-
-        def quantise_x(g, q, t0, t1):
-            quantise(
-                x_codes[:, g, q, t0:t1, :].rearrange("p t m -> p (t m)"),
-                x_planes[:, g, q, t0:t1, :].rearrange("p t m -> p (t m)"),
-                x_grouped[g][:, q, t0:t1, :, :].rearrange("p t m k -> p (t m k)"),
+            nc.vector.tensor_tensor(
+                out=x_grouped[j // 4][:, j % 4, :, :, :].rearrange("p q m (u e) -> p q m u e", e=2),
+                in0=src,
+                in1=x_scales[:].rearrange("p q (u e) -> p q u e", e=2).unsqueeze(2).to_broadcast([P, PASSES, P, 2, 2]),
+                op=MULT,
             )
-            if t1 == 4 and q == PASSES - 1:
-                x_done.add(g)
 
-        units = [(0, 0), (1, 0), (0, 1), (1, 1), (0, 2), (0, 3), (1, 2), (1, 3)]
-        blocks = [(h, g, k) for h, g in units for k in range(2)]
+        def quantise_x(j0, j1):
+            part = x_grouped[j0 // 4][:, j0 % 4 : (j1 - 1) % 4 + 1, :, :, :]
+            quantise(
+                x_codes[:, j0:j1, :, :].rearrange("p j q m -> p (j q m)"),
+                x_planes[:, j0:j1, :, :].rearrange("p j q m -> p (j q m)"),
+                part.rearrange("p j q m t -> p (j q m t)"),
+            )
+
+        blocks = [(h, g, k) for h, g in UNITS for k in range(2)]
+        last = len(blocks) - 1
         banks = {}
         members = {}
         a_grouped = {}
@@ -162,95 +150,43 @@ def tile_soft_cluster_centres_s7_kernel(tc, x_bytes, x_scale, c, b, mass, v, mem
             h, g, k = blocks[i]
             return slice(h * HALF + k * CHUNK, h * HALF + (k + 1) * CHUNK)
 
-        def score(i, pair):
+        def score(i):
             h, g, k = blocks[i]
-            if KINDS[i] == "t":
-                bank = work.tile([P, 4 * P], F32, name="bank")
-                cols = slice(h * HALF + k * CHUNK + pair * P, h * HALF + k * CHUNK + (pair + 1) * P)
-                for q in range(PASSES):
-                    nc.tensor.matmul_mx(
-                        out=bank[:],
-                        lhsT=c_codes[:, q, cols].bitcast(FP8X4),
-                        lhsT_scale=c_planes[:, q, cols],
-                        rhs=x_codes[:, g, q, :, :].rearrange("p t m -> p (t m)").bitcast(FP8X4),
-                        rhs_scale=x_planes[:, g, q, :, :].rearrange("p t m -> p (t m)"),
-                        start=(q == 0),
-                        stop=(q == PASSES - 1),
-                    )
-            else:
-                bank = work.tile([P, 2, CHUNK], F32, name="bank")
+            for pair in range(2):
+                bank = psum.tile([P, 2, CHUNK], F32, name="bank")
                 for s in range(2):
+                    j = 4 * g + 2 * pair + s
                     for q in range(PASSES):
                         nc.tensor.matmul_mx(
                             out=bank[:, s, :],
-                            lhsT=x_codes[:, g, q, 2 * pair + s, :].bitcast(FP8X4),
-                            lhsT_scale=x_planes[:, g, q, 2 * pair + s, :],
-                            rhs=c_codes[:, q, chunk_cols(i)].bitcast(FP8X4),
-                            rhs_scale=c_planes[:, q, chunk_cols(i)],
+                            lhsT=x_codes[:, j, q, :].bitcast(FP8X4),
+                            lhsT_scale=x_planes[:, j, q, :],
+                            rhs=c_codes[:, h, q, k * CHUNK : (k + 1) * CHUNK].bitcast(FP8X4),
+                            rhs_scale=c_planes[:, h, q, k * CHUNK : (k + 1) * CHUNK],
                             start=(q == 0),
                             stop=(q == PASSES - 1),
                         )
-            banks[i, pair] = bank
-
-        flipped = {}
-        returned = {}
-
-        def squash_flipped(i, pair):
-            h, g, k = blocks[i]
-            r = 4 * h + 2 * k + pair
-            flipped[i, pair] = flip.tile([P, 4 * P], F32, name="flipped")
-            nc.scalar.activation(out=flipped[i, pair][:], in_=banks[i, pair][:], func=SIGMOID, bias=b_cols[:, r : r + 1])
-
-        def turn_back(i, pair):
-            bank = work.tile([P, 4, P], F32, name="bank")
-            for t in range(4):
-                nc.tensor.transpose(bank[:, t, :], flipped[i, pair][:, t * P : (t + 1) * P], ident[:])
-            returned[i, pair] = bank
-
-        def member_tile(i):
-            if i // 2 not in members:
-                members[i // 2] = zp.tile([P, 4, HALF], F32, name="member")
-            return members[i // 2]
-
-        def a_tile(i):
-            if i // 2 not in a_grouped:
-                a_grouped[i // 2] = agp.tile([P, HALF, 4], BF16, name="a_grouped", align_bytes=64)
-            return a_grouped[i // 2]
-
-        def keep_member(i, pair, eng):
-            k = blocks[i][2]
-            cols = slice(k * CHUNK + pair * P, k * CHUNK + (pair + 1) * P)
-            if eng == "s":
-                nc.scalar.copy(out=member_tile(i)[:, :, cols], in_=returned[i, pair][:])
-            else:
-                nc.vector.tensor_copy(out=member_tile(i)[:, :, cols], in_=returned[i, pair][:])
-
-        def weigh_returned(i, pair):
-            h, g, k = blocks[i]
-            n = k * CHUNK + pair * P
-            nc.vector.tensor_tensor(
-                out=a_tile(i)[:, n : n + P, :],
-                in0=returned[i, pair][:].rearrange("p t n -> p n t"),
-                in1=masses[:, g, :].unsqueeze(1).to_broadcast([P, P, 4]),
-                op=MULT,
-            )
+                banks[i, pair] = bank
 
         def unit_slice(i, t0, t1):
             k = blocks[i][2]
             return members[i // 2][:, t0:t1, k * CHUNK : (k + 1) * CHUNK]
 
-        def add_bias(i, pair):
-            member_tile(i)
-            nc.vector.tensor_tensor(
-                out=unit_slice(i, 2 * pair, 2 * pair + 2),
-                in0=banks[i, pair][:],
-                in1=b_all[:, chunk_cols(i)].unsqueeze(1).to_broadcast([P, 2, CHUNK]),
-                op=ADD,
-            )
+        def add_bias(i):
+            if i % 2 == 0:
+                members[i // 2] = zp.tile([P, 4, HALF], F32, name="member")
+            for pair in range(2):
+                nc.vector.tensor_tensor(
+                    out=unit_slice(i, 2 * pair, 2 * pair + 2),
+                    in0=banks[i, pair][:],
+                    in1=b_all[:, chunk_cols(i)].unsqueeze(1).to_broadcast([P, 2, CHUNK]),
+                    op=ADD,
+                )
 
-        def squash(i, pair=None):
-            z = unit_slice(i, 0, 4) if pair is None else unit_slice(i, 2 * pair, 2 * pair + 2)
-            nc.scalar.activation(out=z, in_=z, func=SIGMOID)
+        def squash(i, parts):
+            for n in range(parts):
+                z = unit_slice(i, 4 * n // parts, 4 * (n + 1) // parts)
+                nc.scalar.activation(out=z, in_=z, func=SIGMOID)
 
         def store_member(i, whole):
             h, g, k = blocks[i]
@@ -262,7 +198,8 @@ def tile_soft_cluster_centres_s7_kernel(tc, x_bytes, x_scale, c, b, mass, v, mem
 
         def weigh(i):
             h, g, k = blocks[i]
-            a_tile(i)
+            if i // 2 not in a_grouped:
+                a_grouped[i // 2] = agp.tile([P, HALF, 4], BF16, name="a_grouped", align_bytes=64)
             eng = nc.vector if KINDS[i] == "v" else nc.gpsimd
             width = CHUNK if KINDS[i] == "v" else WEIGH_COLS
             for n in range(k * CHUNK, (k + 1) * CHUNK, width):
@@ -285,7 +222,7 @@ def tile_soft_cluster_centres_s7_kernel(tc, x_bytes, x_scale, c, b, mass, v, mem
 
         def centre(h, g, r):
             if g == 0:
-                centres[h, r] = sums.tile([P, D], F32, name=f"centre{r}")
+                centres[h, r] = psum.tile([P, D], F32, name="bank")
             cols = slice(h * HALF + r * P, h * HALF + (r + 1) * P)
             nc.tensor.matmul_mx(
                 out=centres[h, r][:],
@@ -313,167 +250,103 @@ def tile_soft_cluster_centres_s7_kernel(tc, x_bytes, x_scale, c, b, mass, v, mem
             load_x(0, 2, 4)
             load_c(0, 0)
             load_c(1, 0)
-            nc.vector.memset(b_eight[:], 0.0)
-            nc.scalar.dma_start(out=b_eight[0:8, :], in_=b.rearrange("(r p) -> r p", p=P))
             nc.scalar.dma_start(out=masses[:], in_=mass.rearrange("(g p t) -> p g t", p=P, t=4))
             make_identity(nc, ident[:])
-            nc.gpsimd.tensor_copy(out=ident_bf[:], in_=ident[:])
             load_x(1, 0, 4)
             load_c(0, 1)
             load_c(1, 1)
+            nc.sync.dma_start(out=b_all[:], in_=b.partition_broadcast(P))
             load_v(0)
             load_x(2, 0, 4)
             load_v(1)
             load_x(3, 0, 4)
             load_v(2)
             load_v(3)
-            nc.sync.dma_start(out=b_all[:], in_=b.partition_broadcast(P))
 
-            fills = [("x", j) for j in range(4)] + [("b",)] + [("x", 4)]
-            fills += [("s", 0, 0), ("s", 0, 1)]
-            for i in range(16):
-                fills += [("x", j) for j in X_STEPS[i]]
-                if KINDS[i] == "t":
-                    fills += [("r", i, 0), ("r", i, 1)]
-                if i + 1 < 16:
-                    fills += [("s", i + 1, 0), ("s", i + 1, 1)]
-            pending = list(fills)
+            widened = [0]
 
-            def may_fill(what):
-                n = len(fills) - len(pending)
-                if n >= 4 and fills[n - 4] not in taken:
-                    return False
-                if what[0] == "x":
-                    return what[1] in x_wide
-                if what[0] == "s":
-                    h, g, k = blocks[what[1]]
-                    return g in x_done and 2 * h + 1 in c_done
-                if what[0] == "r":
-                    return (what[1], what[2]) in flipped
-                return True
-
-            def fill():
-                while pending and may_fill(pending[0]):
-                    what = pending[0]
-                    pending.remove(what)
-                    if what[0] == "x":
-                        turn(what[1])
-                    elif what[0] == "b":
-                        spread_b()
-                    elif what[0] == "s":
-                        score(what[1], what[2])
-                    else:
-                        turn_back(what[1], what[2])
-
-            def took(*what):
-                taken.add(what)
-                fill()
-
-            def take_x(j):
-                scale_x(j)
-                took("x", j)
-
-            x_ahead = [j for js in X_STEPS for j in js]
-
-            def widen_next():
-                if x_ahead:
-                    widen(x_ahead[0])
-                    x_ahead.remove(x_ahead[0])
-                    fill()
+            def widen_to(n):
+                while widened[0] < min(n, 16):
+                    widen(widened[0])
+                    widened[0] += 1
 
             for j in range(4):
-                widen(j)
-                fill()
-            take_x(0)
-            take_x(1)
+                widen_to(j + 1)
+                turn(j)
             c_grouped = [interleave(C_ENGINES[n], c_raw[n % 2][n // 2]) for n in range(2)]
-            take_x(2)
+            scale_x(0)
+            scale_x(1)
+            widen_to(5)
+            turn(4)
             quantise_c(0, 0, c_grouped[0])
-            take_x(3)
-            widen(4)
-            widen_next()
-            c_grouped.append(interleave(C_ENGINES[2], c_raw[0][1]))
-            quantise_x(0, 0, 0, 4)
+            quantise_x(0, 2)
+            scale_x(2)
+            scale_x(3)
             quantise_c(1, 0, c_grouped[1])
-            quantise_x(0, 1, 0, 4)
-            fill()
-            take_x(4)
-            widen_next()
-            v_grouped = {0: interleave(V_ENGINES[0], v_raw[0])}
-            if KINDS[0] == "t":
-                for pair in range(2):
-                    squash_flipped(0, pair)
-                    took("s", 0, pair)
-            c_grouped.append(interleave(C_ENGINES[3], c_raw[1][1]))
+            quantise_x(2, 4)
+            scale_x(4)
+            c_grouped += [interleave(C_ENGINES[n], c_raw[n % 2][n // 2]) for n in range(2, 4)]
+            v_grouped = []
+            widen_to(6)
+            turn(5)
+            score(0)
 
             for i in range(len(blocks)):
                 h, g, k = blocks[i]
-                kind = KINDS[i]
+                if i >= 1:
+                    squash(i - 1, 1 if i - 1 < 12 else 2)
+                if i < last:
+                    for j in X_STEPS[i + 1]:
+                        widen_to(j + 1)
+                        turn(j)
                 for j in X_STEPS[i]:
-                    take_x(j)
-                    if j % 4 == 3:
-                        for q in range(PASSES):
-                            quantise_x(j // 4, q, 0, 4)
-                        fill()
-                    widen_next()
-                if kind == "t":
-                    weigh_returned(i, 0)
-                    keep_member(i, 1, "s")
-                    keep_member(i, 0, "s")
-                    took("r", i, 0)
-                    weigh_returned(i, 1)
-                    took("r", i, 1)
-                else:
-                    if i + 1 < 16 and KINDS[i + 1] == "t" and not X_STEPS[i]:
-                        for pair in range(2):
-                            squash_flipped(i + 1, pair)
-                            took("s", i + 1, pair)
-                    for pair in range(2):
-                        add_bias(i, pair)
-                        took("s", i, pair)
-                        squash(i, pair)
+                    scale_x(j)
+                add_bias(i)
+                if i == last:
+                    squash(i, 2)
                 if i == 0:
                     quantise_c(0, 1, c_grouped[2])
                     quantise_c(1, 1, c_grouped[3])
-                    fill()
-                if i + 1 < 16 and KINDS[i + 1] == "t" and (kind == "t" or X_STEPS[i]):
-                    for pair in range(2):
-                        squash_flipped(i + 1, pair)
-                        took("s", i + 1, pair)
-                if i >= 1 and KINDS[i - 1] == "v":
-                    weigh(i - 1)
-                if i in (1, 3, 5, 7):
-                    n = i // 2
+                if X_STEPS[i] and X_STEPS[i][-1] % 4 == 3:
+                    quantise_x(X_STEPS[i][-1] - 3, X_STEPS[i][-1] + 1)
+                elif len(X_STEPS[i]) == 2 and X_STEPS[i][0] % 4 == 3:
+                    quantise_x(X_STEPS[i][0] - 3, X_STEPS[i][0] + 1)
+                if i < last:
+                    score(i + 1)
+                    widen_to(i + 9)
+                w = i - 1
+                if w >= 0:
+                    weigh(w)
+                if w >= 0 and w < 14 and blocks[w][2] == 1:
+                    store_member(w, True)
+                if w >= 14:
+                    store_member(w, False)
+                if i in V_STEPS:
+                    n = len(v_grouped)
+                    v_grouped.append(interleave(V_ENGINES[n], v_raw[n]))
+                if i - 1 in V_STEPS:
+                    n = V_STEPS.index(i - 1)
                     quantise_v(n, v_grouped[n])
-                    if n + 1 < GROUPS:
-                        v_grouped[n + 1] = interleave(V_ENGINES[n + 1], v_raw[n + 1])
-                if i < 14 and k == 1:
-                    store_member(i, True)
-                if i >= 14:
-                    store_member(i, False)
-                u = i // 2 - 1
-                if i >= 2 and i % 2 == 0:
+                u = A_UNIT[i]
+                if u >= 0:
                     quantise_a(2 * u, True)
-                if i >= 3 and i % 2 == 1:
-                    if units[u][0] == 0:
-                        for r in range(4):
-                            centre(0, units[u][1], r)
-                            if u == 5:
-                                finish(0, r, FINISH[r])
-                if i == 14:
-                    for g2 in range(2):
-                        for r in range(4):
-                            centre(1, g2, r)
-                if i == 15:
+                for r in H0_STEPS.get(i, ()):
+                    for g2 in range(GROUPS):
+                        centre(0, g2, r)
+                if i == last:
                     for r in range(4):
-                        centre(1, 2, r)
-                    quantise_a(14, False)
-                    for r in range(2):
-                        centre(1, GROUPS - 1, r)
-                        finish(1, r, FINISH[4 + r])
-            if KINDS[15] == "v":
-                weigh(15)
-            quantise_a(15, False)
-            for r in range(2, 4):
-                centre(1, GROUPS - 1, r)
+                        finish(0, r, FINISH[r])
+                if i == last:
+                    for r in range(4):
+                        for g2 in range(3):
+                            centre(1, g2, r)
+            store_member(last, False)
+            quantise_a(last - 1, False)
+            for r in range(2):
+                centre(1, 3, r)
+            weigh(last)
+            quantise_a(last, False)
+            for r in range(4):
+                if r >= 2:
+                    centre(1, 3, r)
                 finish(1, r, FINISH[4 + r])

@@ -24,15 +24,15 @@ HALF = 512
 CHUNK = 256
 KINDS = "gggggggggggvgvgv"
 WEIGH_COLS = 128
-IL_COLS = 512
+IL_COLS = 128
 C_ENGINES = ("v", "g", "s", "g")
 V_ENGINES = ("s", "s", "s", "s")
 UNITS = ((0, 0), (1, 0), (0, 1), (1, 1), (0, 2), (0, 3), (1, 2), (1, 3))
 X_STEPS = ((5,), (6,), (7,), (8,), (9,), (10,), (11,), (12, 13), (14, 15)) + ((),) * 7
 V_STEPS = (3, 7, 8, 9)
-H0_STEPS = {13: (0,), 14: (1,), 15: (2, 3)}
+H0_STEPS = {14: (0, 1), 15: (2, 3)}
 BANKS = 8
-FINISH = "ssssssvs"
+FINISH = "sssvsvvs"
 A_UNIT = (-1, -1, -1, -1, 0, -1, 1, -1, 2, -1, 3, -1, 4, 5, -1, 6)
 
 
@@ -201,7 +201,7 @@ def tile_soft_cluster_centres_s7_kernel(tc, x_bytes, x_scale, c, b, mass, v, mem
             if i // 2 not in a_grouped:
                 a_grouped[i // 2] = agp.tile([P, HALF, 4], BF16, name="a_grouped", align_bytes=64)
             eng = nc.vector if KINDS[i] == "v" else nc.gpsimd
-            width = CHUNK if KINDS[i] == "v" else WEIGH_COLS
+            width = CHUNK if KINDS[i] == "v" and i < last else WEIGH_COLS
             for n in range(k * CHUNK, (k + 1) * CHUNK, width):
                 eng.tensor_tensor(
                     out=a_grouped[i // 2][:, n : n + width, :].rearrange("p (n i) t -> p n t i", i=4),
@@ -243,14 +243,15 @@ def tile_soft_cluster_centres_s7_kernel(tc, x_bytes, x_scale, c, b, mass, v, mem
             nc.sync.dma_start(out=centre_out[h * HALF + r * P : h * HALF + (r + 1) * P, :], in_=result[:])
 
         with tc.manual_schedule():
-            nc.vector.memset(spark[:], 0.0)
-            nc.scalar.activation(out=spark[:], in_=spark[:], func=SIGMOID)
-            load_x(0, 0, 2)
-            nc.sync.dma_start(out=x_scales[:], in_=x_scale.rearrange("o (q p t) -> p (o q) t", p=P, t=4))
+            load_x(0, 0, 1)
+            load_x(0, 1, 2)
             load_x(0, 2, 4)
             load_c(0, 0)
             load_c(1, 0)
+            nc.scalar.dma_start(out=x_scales[:], in_=x_scale.rearrange("o (q p t) -> p (o q) t", p=P, t=4))
             nc.scalar.dma_start(out=masses[:], in_=mass.rearrange("(g p t) -> p g t", p=P, t=4))
+            nc.vector.memset(spark[:], 0.0)
+            nc.scalar.activation(out=spark[:], in_=spark[:], func=SIGMOID)
             make_identity(nc, ident[:])
             load_x(1, 0, 4)
             load_c(0, 1)
@@ -345,8 +346,9 @@ def tile_soft_cluster_centres_s7_kernel(tc, x_bytes, x_scale, c, b, mass, v, mem
             for r in range(2):
                 centre(1, 3, r)
             weigh(last)
-            quantise_a(last, False)
+            for r in range(2, 4):
+                cols = slice(HALF + r * P, HALF + (r + 1) * P)
+                quantise(a_codes[:, 3, cols], a_planes[:, 3, cols], a_grouped[last // 2][:, r * P : (r + 1) * P, :].rearrange("p n t -> p (n t)"))
+                centre(1, 3, r)
             for r in range(4):
-                if r >= 2:
-                    centre(1, 3, r)
                 finish(1, r, FINISH[4 + r])

from contextlib import ExitStack

import concourse.mybir as mybir
from concourse.masks import make_identity

M, K, R, D = 2048, 1024, 1024, 512
FLOPS = 2 * M * K * R + 2 * M * R * D

F32 = mybir.dt.float32
BF16 = mybir.dt.bfloat16
U32 = mybir.dt.uint32
U8 = mybir.dt.uint8
FP8 = mybir.dt.float8_e4m3fn
FP8X4 = mybir.dt.float8_e4m3fn_x4
MULT = mybir.AluOpType.mult
ADD = mybir.AluOpType.add
SIGMOID = mybir.ActivationFunctionType.Sigmoid

P = 128
GROUP = 512
GROUPS = M // GROUP
PASSES = K // 512
HALF = 512
CHUNK = 256
KINDS = "gggggggggggvgvgv"
WEIGH_COLS = 128
IL_COLS = 128
C_ENGINES = ("v", "g", "s", "g")
V_ENGINES = ("s", "s", "s", "s")
UNITS = ((0, 0), (1, 0), (0, 1), (1, 1), (0, 2), (0, 3), (1, 2), (1, 3))
X_STEPS = ((5,), (6,), (7,), (8,), (9,), (10,), (11,), (12, 13), (14, 15)) + ((),) * 7
V_STEPS = (3, 7, 8, 9)
H0_STEPS = {14: (0, 1), 15: (2, 3)}
BANKS = 8
FINISH = "sssvsvvs"
A_UNIT = (-1, -1, -1, -1, 0, -1, 1, -1, 2, -1, 3, -1, 4, 5, -1, 6)


def tile_soft_cluster_centres_s7_kernel(tc, x_bytes, x_scale, c, b, mass, v, member_out, centre_out):
    nc = tc.nc
    with ExitStack() as ctx:
        keep = ctx.enter_context(tc.tile_pool(name="keep", bufs=1))
        wide = ctx.enter_context(tc.tile_pool(name="wide", bufs=6))
        xgp = ctx.enter_context(tc.tile_pool(name="xgp", bufs=2))
        cvp = ctx.enter_context(tc.tile_pool(name="cvp", bufs=6))
        agp = ctx.enter_context(tc.tile_pool(name="agp", bufs=3))
        zp = ctx.enter_context(tc.tile_pool(name="zp", bufs=5))
        outp = ctx.enter_context(tc.tile_pool(name="outp", bufs=8))
        psum = ctx.enter_context(tc.psum_pool(name="psum", bufs=BANKS))

        x_raw = [keep.tile([P, 4, K], U8, name=f"x_raw{g}", align_bytes=64) for g in range(GROUPS)]
        c_raw = [[keep.tile([P, 4, HALF], BF16, name=f"c_raw{q}{h}", align_bytes=64) for h in range(2)] for q in range(PASSES)]
        v_raw = [keep.tile([P, 4, D], BF16, name=f"v_raw{g}", align_bytes=64) for g in range(GROUPS)]
        x_codes = keep.tile([P, 4 * GROUPS, PASSES, P], U32, name="x_codes", align_bytes=64)
        x_planes = keep.tile([P, 4 * GROUPS, PASSES, P], U8, name="x_planes", align_bytes=64)
        c_codes = keep.tile([P, 2, PASSES, HALF], U32, name="c_codes", align_bytes=64)
        c_planes = keep.tile([P, 2, PASSES, HALF], U8, name="c_planes", align_bytes=64)
        v_codes = keep.tile([P, GROUPS, D], U32, name="v_codes", align_bytes=64)
        v_planes = keep.tile([P, GROUPS, D], U8, name="v_planes", align_bytes=64)
        a_codes = keep.tile([P, GROUPS, R], U32, name="a_codes", align_bytes=64)
        a_planes = keep.tile([P, GROUPS, R], U8, name="a_planes", align_bytes=64)
        x_scales = keep.tile([P, PASSES, 4], F32, name="x_scales")
        masses = keep.tile([P, GROUPS, 4], BF16, name="masses")
        b_all = keep.tile([P, R], BF16, name="b_all")
        ident = keep.tile([P, P], F32, name="ident")
        spark = keep.tile([P, 1], F32, name="spark")

        def load_x(g, t0, t1):
            rows = x_bytes[g * GROUP : (g + 1) * GROUP, :].rearrange("(p t) k -> p t k", t=4)
            nc.sync.dma_start(out=x_raw[g][:, t0:t1, :], in_=rows[:, t0:t1, :])

        def load_c(q, h):
            rows = c[q * 512 : (q + 1) * 512, h * HALF : (h + 1) * HALF].rearrange("(p t) n -> p t n", t=4)
            nc.sync.dma_start(out=c_raw[q][h][:], in_=rows)

        def load_v(g):
            nc.sync.dma_start(out=v_raw[g][:], in_=v[g * GROUP : (g + 1) * GROUP, :].rearrange("(p t) n -> p t n", t=4))

        def interleave(eng, raw):
            grouped = cvp.tile([P, 512, 4], BF16, name="cv_grouped", align_bytes=64)
            width = IL_COLS if eng == "g" else 512
            for n in range(0, 512, width):
                if eng == "g":
                    src = raw[:, :, n : n + width].rearrange("p t n -> p n t")
                    dst = grouped[:, n : n + width, :]
                else:
                    src = raw[:, :, n : n + width].rearrange("p t (n i) -> p n t i", i=4)
                    dst = grouped[:, n : n + width, :].rearrange("p (n i) t -> p n t i", i=4)
                if eng == "v":
                    nc.vector.tensor_copy(out=dst, in_=src)
                elif eng == "s":
                    nc.scalar.copy(out=dst, in_=src)
                else:
                    nc.gpsimd.tensor_scalar(out=dst, in0=src, scalar1=1.0, scalar2=0.0, op0=MULT, op1=ADD)
            return grouped

        def quantise(codes, planes, grouped):
            nc.vector.quantize_mx(out=codes.bitcast(FP8X4), scales=planes, in_=grouped)

        def quantise_c(q, h, grouped):
            quantise(c_codes[:, h, q, :], c_planes[:, h, q, :], grouped[:].rearrange("p n t -> p (n t)"))

        def quantise_v(g, grouped):
            quantise(v_codes[:, g, :], v_planes[:, g, :], grouped[:].rearrange("p n t -> p (n t)"))

        x_wide = {}
        x_turned = {}
        x_grouped = {}

        def widen(j):
            g, t = j // 4, j % 4
            x_wide[j] = wide.tile([P, K], BF16, name="x_wide")
            nc.scalar.copy(out=x_wide[j][:], in_=x_raw[g][:, t, :].bitcast(FP8))

        def turn(j):
            words = x_wide[j][:].bitcast(F32)
            bank = psum.tile([P, 2, PASSES, P], F32, name="bank")
            for u in range(2):
                for q in range(PASSES):
                    nc.tensor.transpose(bank[:, u, q, :], words[:, q * 256 + u : (q + 1) * 256 : 2], ident[:])
            x_turned[j] = bank

        def scale_x(j):
            if j % 4 == 0:
                x_grouped[j // 4] = xgp.tile([P, 4, PASSES, P, 4], BF16, name="x_grouped", align_bytes=64)
            src = x_turned[j][:].bitcast(BF16).rearrange("p u q (m e) -> p q m u e", e=2)
            nc.vector.tensor_tensor(
                out=x_grouped[j // 4][:, j % 4, :, :, :].rearrange("p q m (u e) -> p q m u e", e=2),
                in0=src,
                in1=x_scales[:].rearrange("p q (u e) -> p q u e", e=2).unsqueeze(2).to_broadcast([P, PASSES, P, 2, 2]),
                op=MULT,
            )

        def quantise_x(j0, j1):
            part = x_grouped[j0 // 4][:, j0 % 4 : (j1 - 1) % 4 + 1, :, :, :]
            quantise(
                x_codes[:, j0:j1, :, :].rearrange("p j q m -> p (j q m)"),
                x_planes[:, j0:j1, :, :].rearrange("p j q m -> p (j q m)"),
                part.rearrange("p j q m t -> p (j q m t)"),
            )

        blocks = [(h, g, k) for h, g in UNITS for k in range(2)]
        last = len(blocks) - 1
        banks = {}
        members = {}
        a_grouped = {}
        centres = {}

        def chunk_cols(i):
            h, g, k = blocks[i]
            return slice(h * HALF + k * CHUNK, h * HALF + (k + 1) * CHUNK)

        def score(i):
            h, g, k = blocks[i]
            for pair in range(2):
                bank = psum.tile([P, 2, CHUNK], F32, name="bank")
                for s in range(2):
                    j = 4 * g + 2 * pair + s
                    for q in range(PASSES):
                        nc.tensor.matmul_mx(
                            out=bank[:, s, :],
                            lhsT=x_codes[:, j, q, :].bitcast(FP8X4),
                            lhsT_scale=x_planes[:, j, q, :],
                            rhs=c_codes[:, h, q, k * CHUNK : (k + 1) * CHUNK].bitcast(FP8X4),
                            rhs_scale=c_planes[:, h, q, k * CHUNK : (k + 1) * CHUNK],
                            start=(q == 0),
                            stop=(q == PASSES - 1),
                        )
                banks[i, pair] = bank

        def unit_slice(i, t0, t1):
            k = blocks[i][2]
            return members[i // 2][:, t0:t1, k * CHUNK : (k + 1) * CHUNK]

        def add_bias(i):
            if i % 2 == 0:
                members[i // 2] = zp.tile([P, 4, HALF], F32, name="member")
            for pair in range(2):
                nc.vector.tensor_tensor(
                    out=unit_slice(i, 2 * pair, 2 * pair + 2),
                    in0=banks[i, pair][:],
                    in1=b_all[:, chunk_cols(i)].unsqueeze(1).to_broadcast([P, 2, CHUNK]),
                    op=ADD,
                )

        def squash(i, parts):
            for n in range(parts):
                z = unit_slice(i, 4 * n // parts, 4 * (n + 1) // parts)
                nc.scalar.activation(out=z, in_=z, func=SIGMOID)

        def store_member(i, whole):
            h, g, k = blocks[i]
            rows = member_out[g * GROUP : (g + 1) * GROUP, :].rearrange("(p t) n -> p t n", t=4)
            if whole:
                nc.sync.dma_start(out=rows[:, :, h * HALF : (h + 1) * HALF], in_=members[i // 2][:])
            else:
                nc.sync.dma_start(out=rows[:, :, chunk_cols(i)], in_=unit_slice(i, 0, 4))

        def weigh(i):
            h, g, k = blocks[i]
            if i // 2 not in a_grouped:
                a_grouped[i // 2] = agp.tile([P, HALF, 4], BF16, name="a_grouped", align_bytes=64)
            eng = nc.vector if KINDS[i] == "v" else nc.gpsimd
            width = CHUNK if KINDS[i] == "v" and i < last else WEIGH_COLS
            for n in range(k * CHUNK, (k + 1) * CHUNK, width):
                eng.tensor_tensor(
                    out=a_grouped[i // 2][:, n : n + width, :].rearrange("p (n i) t -> p n t i", i=4),
                    in0=members[i // 2][:, :, n : n + width].rearrange("p t (n i) -> p n t i", i=4),
                    in1=masses[:, g, :].unsqueeze(1).unsqueeze(3).to_broadcast([P, width // 4, 4, 4]),
                    op=MULT,
                )

        def quantise_a(i, whole):
            h, g, k = blocks[i]
            if whole:
                cols = slice(h * HALF, (h + 1) * HALF)
                part = a_grouped[i // 2][:]
            else:
                cols = chunk_cols(i)
                part = a_grouped[i // 2][:, k * CHUNK : (k + 1) * CHUNK, :]
            quantise(a_codes[:, g, cols], a_planes[:, g, cols], part.rearrange("p n t -> p (n t)"))

        def centre(h, g, r):
            if g == 0:
                centres[h, r] = psum.tile([P, D], F32, name="bank")
            cols = slice(h * HALF + r * P, h * HALF + (r + 1) * P)
            nc.tensor.matmul_mx(
                out=centres[h, r][:],
                lhsT=a_codes[:, g, cols].bitcast(FP8X4),
                lhsT_scale=a_planes[:, g, cols],
                rhs=v_codes[:, g, :].bitcast(FP8X4),
                rhs_scale=v_planes[:, g, :],
                start=(g == 0),
                stop=(g == GROUPS - 1),
            )

        def finish(h, r, eng):
            result = outp.tile([P, D], F32, name="result")
            if eng == "s":
                nc.scalar.copy(out=result[:], in_=centres[h, r][:])
            else:
                nc.vector.tensor_copy(out=result[:], in_=centres[h, r][:])
            nc.sync.dma_start(out=centre_out[h * HALF + r * P : h * HALF + (r + 1) * P, :], in_=result[:])

        with tc.manual_schedule():
            load_x(0, 0, 1)
            load_x(0, 1, 2)
            load_x(0, 2, 4)
            load_c(0, 0)
            load_c(1, 0)
            nc.scalar.dma_start(out=x_scales[:], in_=x_scale.rearrange("o (q p t) -> p (o q) t", p=P, t=4))
            nc.scalar.dma_start(out=masses[:], in_=mass.rearrange("(g p t) -> p g t", p=P, t=4))
            nc.vector.memset(spark[:], 0.0)
            nc.scalar.activation(out=spark[:], in_=spark[:], func=SIGMOID)
            make_identity(nc, ident[:])
            load_x(1, 0, 4)
            load_c(0, 1)
            load_c(1, 1)
            nc.sync.dma_start(out=b_all[:], in_=b.partition_broadcast(P))
            load_v(0)
            load_x(2, 0, 4)
            load_v(1)
            load_x(3, 0, 4)
            load_v(2)
            load_v(3)

            widened = [0]

            def widen_to(n):
                while widened[0] < min(n, 16):
                    widen(widened[0])
                    widened[0] += 1

            for j in range(4):
                widen_to(j + 1)
                turn(j)
            c_grouped = [interleave(C_ENGINES[n], c_raw[n % 2][n // 2]) for n in range(2)]
            scale_x(0)
            scale_x(1)
            widen_to(5)
            turn(4)
            quantise_c(0, 0, c_grouped[0])
            quantise_x(0, 2)
            scale_x(2)
            scale_x(3)
            quantise_c(1, 0, c_grouped[1])
            quantise_x(2, 4)
            scale_x(4)
            c_grouped += [interleave(C_ENGINES[n], c_raw[n % 2][n // 2]) for n in range(2, 4)]
            v_grouped = []
            widen_to(6)
            turn(5)
            score(0)

            for i in range(len(blocks)):
                h, g, k = blocks[i]
                if i >= 1:
                    squash(i - 1, 1 if i - 1 < 12 else 2)
                if i < last:
                    for j in X_STEPS[i + 1]:
                        widen_to(j + 1)
                        turn(j)
                for j in X_STEPS[i]:
                    scale_x(j)
                add_bias(i)
                if i == last:
                    squash(i, 2)
                if i == 0:
                    quantise_c(0, 1, c_grouped[2])
                    quantise_c(1, 1, c_grouped[3])
                if X_STEPS[i] and X_STEPS[i][-1] % 4 == 3:
                    quantise_x(X_STEPS[i][-1] - 3, X_STEPS[i][-1] + 1)
                elif len(X_STEPS[i]) == 2 and X_STEPS[i][0] % 4 == 3:
                    quantise_x(X_STEPS[i][0] - 3, X_STEPS[i][0] + 1)
                if i < last:
                    score(i + 1)
                    widen_to(i + 9)
                w = i - 1
                if w >= 0:
                    weigh(w)
                if w >= 0 and w < 14 and blocks[w][2] == 1:
                    store_member(w, True)
                if w >= 14:
                    store_member(w, False)
                if i in V_STEPS:
                    n = len(v_grouped)
                    v_grouped.append(interleave(V_ENGINES[n], v_raw[n]))
                if i - 1 in V_STEPS:
                    n = V_STEPS.index(i - 1)
                    quantise_v(n, v_grouped[n])
                u = A_UNIT[i]
                if u >= 0:
                    quantise_a(2 * u, True)
                for r in H0_STEPS.get(i, ()):
                    for g2 in range(GROUPS):
                        centre(0, g2, r)
                if i == last:
                    for r in range(4):
                        finish(0, r, FINISH[r])
                if i == last:
                    for r in range(4):
                        for g2 in range(3):
                            centre(1, g2, r)
            store_member(last, False)
            quantise_a(last - 1, False)
            for r in range(2):
                centre(1, 3, r)
            weigh(last)
            for r in range(2, 4):
                cols = slice(HALF + r * P, HALF + (r + 1) * P)
                quantise(a_codes[:, 3, cols], a_planes[:, 3, cols], a_grouped[last // 2][:, r * P : (r + 1) * P, :].rearrange("p n t -> p (n t)"))
                centre(1, 3, r)
            for r in range(4):
                finish(1, r, FINISH[4 + r])
